import numpy as np
import ml_dtypes


def mxq(x, axis, fmt="e4m3"):
    dtype, down = {"e4m3": (ml_dtypes.float8_e4m3fn, 7), "e5m2": (ml_dtypes.float8_e5m2, 14)}[fmt]
    v = np.moveaxis(np.asarray(x, np.float32).astype(ml_dtypes.bfloat16).astype(np.float64), axis, -1)
    blocks = v.reshape(v.shape[:-1] + (-1, 32))
    amax = np.abs(blocks).max(-1, keepdims=True)
    byte = np.maximum(np.where(amax > 0, np.frexp(amax)[1] - 1 + 127, 0) - down, 1)
    scale = np.exp2(byte - 127.0)
    codes = (blocks / scale).astype(np.float32).astype(dtype).astype(np.float64)
    return np.moveaxis((codes * scale).reshape(v.shape), -1, axis)


WIDE = False


def mx_kscale(k):
    if not WIDE:
        return np.ones(k)
    levels = np.array([10, -10, 5, -5, 0])
    if k % 512:
        return np.exp2(np.random.permutation(np.resize(levels, k // 32))).repeat(32)
    a = np.empty((k // 512, 16))
    for p in range(k // 512):
        a[p, :8] = np.random.permutation(np.resize(levels, 8))
        for g in range(8):
            far = levels[np.abs(levels - a[p, g]) >= 10]
            a[p, g + 8] = far[np.random.randint(len(far))]
    return np.exp2(a.ravel()).repeat(32)


def f64(x):
    return np.asarray(x).astype(np.float64)


def striped(idx):
    return np.tile(idx.reshape(-1, 16).T, (8, 1)).astype(np.uint16)


def unstriped(offs):
    return offs[:16].T.reshape(-1).astype(np.int64)


def striped8(idx):
    return np.concatenate([x.reshape(-1, 16).T for x in idx]).astype(np.uint16)


def runs(offs, k):
    lists = np.stack([offs[16 * r : 16 * r + 16].T.reshape(-1) for r in range(8)]).astype(np.int64)
    return lists[np.arange(k) % 512 // 64]


def pack_weight(w):
    k, n = w.shape
    w = f64(np.asarray(w, np.float32).astype(ml_dtypes.bfloat16)).reshape(k // 32, 32, n)
    amax = np.abs(w).max(1)
    byte = np.clip(np.where(amax > 0, np.frexp(amax)[1] - 1 + 127 - 7, 1), 1, 254)
    scaled = (w * np.exp2(127.0 - byte)[:, None, :]).reshape(k, n).astype(np.float32)
    words = np.ascontiguousarray(scaled.reshape(k // 512, 128, 4, n).transpose(0, 1, 3, 2)).astype(ml_dtypes.float8_e4m3fn).view(np.uint8)
    return words, np.ascontiguousarray(byte.astype(np.uint8).reshape(k // 512, 16, n))


def unpack_weight(words, scales):
    g, p, n, _ = words.shape
    vals = np.ascontiguousarray(words).view(ml_dtypes.float8_e4m3fn).astype(np.float64) * np.repeat(np.exp2(scales.astype(np.float64) - 127.0), 8, axis=1)[..., None]
    return vals.transpose(0, 1, 3, 2).reshape(g * 512, n)


def sigmoid(v):
    return 1.0 / (1.0 + np.exp(-np.maximum(v, -700.0)))


K, T, S, N, H = 512, 2048, 512, 512, 512


def setup_inputs():
    n = np.random.standard_normal
    s = mx_kscale(K)[:, None]
    u = mx_kscale(H)
    packed_xT = pack_weight(n((K, T)) * s)
    return {
        "x_words": packed_xT[0],
        "x_scales": packed_xT[1],
        "w1": (n((K, H)) / np.sqrt(K) / s).astype(np.float32),
        "w2": (n((K, H)) / np.sqrt(K) / s).astype(np.float32),
        "gn": (np.random.uniform(0.5, 1.5, (H, 1)) * u[:, None]).astype(np.float32),
        "w3": (n((H, N)) / np.sqrt(H) / u[:, None]).astype(np.float32),
        "offs": striped(np.random.permutation(T)[:S]),
        "two": striped(np.random.permutation(T)[:S]),
        "n1": striped8(np.stack([np.random.permutation(S) for _ in range(8)])),
        "n2": striped8(np.stack([np.random.permutation(S) for _ in range(8)])),
        "n3": striped8(np.stack([np.random.permutation(S) for _ in range(8)])),
        "n4": striped8(np.stack([np.random.permutation(S) for _ in range(8)])),
    }


def reference(x_words, x_scales, w1, w2, gn, w3, offs, two, n1, n2, n3, n4):
    xq = unpack_weight(x_words, x_scales)[:, unstriped(offs)]
    y = mxq(f64(w1), 0, "e4m3").T @ xq
    x_two = unpack_weight(x_words, x_scales)[:, unstriped(two)]
    d = mxq(f64(w2), 0, "e4m3").T @ x_two
    z = f64(gn) * (0.75 * (y * (d[np.arange(H)[:, None], runs(n2, H)]) - ((y[np.arange(H)[:, None], runs(n1, H)]) * d)))
    h = mxq(f64(w3), 0, "e4m3").T @ mxq(z, 0, "e4m3")
    return h * (sigmoid(h[np.arange(N)[:, None], runs(n3, N)] - (h[np.arange(N)[:, None], runs(n4, N)])))

@@ -1,0 +1,188 @@
+from contextlib import ExitStack
+
+import concourse.mybir as mybir
+
+K, T, S, H, N = 512, 2048, 512, 512, 512
+FLOPS = 2 * S * (K * H + K * H + H * N)
+
+F32 = mybir.dt.float32
+BF16 = mybir.dt.bfloat16
+I32 = mybir.dt.int32
+U32 = mybir.dt.uint32
+U16 = mybir.dt.uint16
+U8 = mybir.dt.uint8
+FP8X4 = mybir.dt.float8_e4m3fn_x4
+MULT = mybir.AluOpType.mult
+SUB = mybir.AluOpType.subtract
+COPY = mybir.ActivationFunctionType.Copy
+SIGMOID = mybir.ActivationFunctionType.Sigmoid
+
+P = 128
+PACK = 4
+GROUP = 16
+HALF = S // 2
+
+
+def tile_picked_twlcrossbcmp_none_p_kernel(
+    tc, x_words, x_scales, w1, w2, gn, w3, offs, two, n1, n2, n3, n4, out
+):
+    nc = tc.nc
+    with ExitStack() as ctx:
+        keep = ctx.enter_context(tc.tile_pool(name="keep", bufs=1))
+        first_banks = ctx.enter_context(tc.psum_pool(name="first_banks", bufs=4))
+        second_banks = ctx.enter_context(tc.psum_pool(name="second_banks", bufs=4))
+
+        def list_tile(name):
+            return keep.tile([P, S // GROUP], U16, name=name)
+
+        offs_sb, two_sb = list_tile("offs_sb"), list_tile("two_sb")
+        n1_sb, n2_sb, n3_sb, n4_sb = list_tile("n1_sb"), list_tile("n2_sb"), list_tile("n3_sb"), list_tile("n4_sb")
+
+        table_words = keep.tile([P, T], U32, align_bytes=64)
+        table_scales = keep.tile([P, T], U8, align_bytes=64)
+        gain = keep.tile([P, PACK], F32)
+        pieces = [2, 2, 1]
+        raw = [
+            [keep.tile([P, PACK, H // pieces[i]], F32, name=f"raw{i}_{k}", align_bytes=64) for k in range(pieces[i])]
+            for i in range(3)
+        ]
+
+        def load_weights(i, w):
+            width = H // pieces[i]
+            for k in range(pieces[i]):
+                nc.sync.dma_start(raw[i][k][:], w.rearrange("(p j) c -> p j c", j=PACK)[:, :, k * width : (k + 1) * width])
+
+        warm = keep.tile([P, 8], F32)
+
+        nc.vector.memset(table_scales[:].bitcast(I32), 0)
+        nc.vector.memset(warm[:, 0:1], 0.0)
+        nc.scalar.activation(out=warm[:, 4:5], in_=warm[:, 0:1], func=SIGMOID)
+
+        nc.sync.dma_start(table_words[:].bitcast(I32), x_words[0].rearrange("p n t -> p (n t)").bitcast(I32))
+        nc.sync.dma_start(offs_sb[:], offs)
+        for q in range(4):
+            nc.scalar.dma_start(
+                table_scales[32 * q : 32 * q + 4, :].bitcast(I32), x_scales[0, 4 * q : 4 * q + 4, :].bitcast(I32)
+            )
+        nc.sync.dma_start(two_sb[:], two)
+        load_weights(0, w1)
+        load_weights(1, w2)
+        nc.sync.dma_start(gain[:], gn.rearrange("(p t) o -> p (t o)", t=PACK))
+        nc.sync.dma_start(n2_sb[:], n2)
+        nc.sync.dma_start(n1_sb[:], n1)
+        load_weights(2, w3)
+        nc.sync.dma_start(n4_sb[:], n4)
+        nc.sync.dma_start(n3_sb[:], n3)
+
+        picked = []
+        for name, lst in (("x_offs", offs_sb), ("x_two", two_sb)):
+            words = keep.tile([P, S], U32, name=name + "_words", align_bytes=64)
+            scales = keep.tile([P, S], U8, name=name + "_scales", align_bytes=64)
+            nc.vector.tensor_copy(words[:], table_words[:].indirect(lst[:]))
+            picked.append((words, scales))
+        for (words, scales), lst in zip(picked, (offs_sb, two_sb)):
+            nc.vector.tensor_copy(scales[:], table_scales[:].indirect(lst[:]))
+
+        dealt = [keep.tile([P, PACK, P, PACK], BF16, name=f"dealt{i}", align_bytes=64) for i in range(3)]
+        w_words = [keep.tile([P, PACK, P], U32, name=f"w_words{i}", align_bytes=64) for i in range(3)]
+        w_scales = [keep.tile([P, PACK, P], U8, name=f"w_scales{i}", align_bytes=64) for i in range(3)]
+
+        def deal(i):
+            count = P // pieces[i]
+            for k in range(pieces[i]):
+                nc.scalar.copy(
+                    dealt[i][:, :, k * count : (k + 1) * count, :].rearrange("p t m j -> p m j t"),
+                    raw[i][k][:].rearrange("p j (m t) -> p m j t", t=PACK),
+                )
+
+        def quantize_weights(i, t0, t1):
+            nc.vector.quantize_mx(
+                out=w_words[i][:, t0:t1, :].rearrange("p t m -> p (t m)").bitcast(FP8X4),
+                scales=w_scales[i][:, t0:t1, :].rearrange("p t m -> p (t m)"),
+                in_=dealt[i][:, t0:t1, :, :].rearrange("p t m j -> p (t m j)"),
+            )
+
+        def product(bank, i, t, words, scales):
+            nc.tensor.matmul_mx(
+                out=bank,
+                lhsT=w_words[i][:, t, :].bitcast(FP8X4),
+                lhsT_scale=w_scales[i][:, t, :],
+                rhs=words.bitcast(FP8X4),
+                rhs_scale=scales,
+                start=True,
+                stop=True,
+            )
+
+        deal(0)
+        quantize_weights(0, 0, PACK)
+        deal(1)
+        quantize_weights(1, 0, 1)
+        quantize_weights(1, 1, 2)
+        quantize_weights(1, 2, PACK)
+
+        y = [keep.tile([P, S], F32, name=f"y{t}") for t in range(PACK)]
+        d = [keep.tile([P, S], F32, name=f"d{t}") for t in range(PACK)]
+        for t in range(PACK):
+            y_bank = first_banks.tile([P, S], F32, name="first_bank")
+            product(y_bank[:], 0, t, picked[0][0][:], picked[0][1][:])
+            nc.scalar.activation(out=y[t][:], in_=y_bank[:], func=COPY, scale=gain[:, t : t + 1])
+            d_bank = first_banks.tile([P, S], F32, name="first_bank")
+            product(d_bank[:], 1, t, picked[1][0][:], picked[1][1][:])
+            nc.scalar.activation(out=d[t][:], in_=d_bank[:], func=COPY, scale=0.75)
+
+        deal(2)
+
+        h = [keep.tile([P, S], F32, name=f"h{t}") for t in range(PACK)]
+        for half in range(2):
+            cols = slice(half * HALF, (half + 1) * HALF)
+            entries = slice(half * HALF // GROUP, (half + 1) * HALF // GROUP)
+            left = keep.tile([P, PACK, HALF], F32, name=f"left{half}")
+            right = keep.tile([P, PACK, HALF], F32, name=f"right{half}")
+            for t in range(PACK):
+                nc.vector.tensor_tensor(left[:, t, :], d[t][:].indirect(n2_sb[:, entries]), y[t][:, cols], MULT)
+                nc.vector.tensor_tensor(right[:, t, :], y[t][:].indirect(n1_sb[:, entries]), d[t][:, cols], MULT)
+            z = keep.tile([P, HALF, PACK], BF16, name=f"z{half}", align_bytes=64)
+            nc.vector.tensor_tensor(
+                z[:].rearrange("p (c i) t -> p c t i", i=4),
+                left[:].rearrange("p t (c i) -> p c t i", i=4),
+                right[:].rearrange("p t (c i) -> p c t i", i=4),
+                SUB,
+            )
+            if half == 0:
+                quantize_weights(2, 0, PACK)
+            z_words = keep.tile([P, HALF], U32, name=f"z_words{half}", align_bytes=64)
+            z_scales = keep.tile([P, HALF], U8, name=f"z_scales{half}", align_bytes=64)
+            nc.vector.quantize_mx(
+                out=z_words[:].bitcast(FP8X4), scales=z_scales[:], in_=z[:].rearrange("p n t -> p (n t)")
+            )
+            for t in range(PACK):
+                h_bank = second_banks.tile([P, HALF], F32, name="second_bank")
+                product(h_bank[:], 2, t, z_words[:], z_scales[:])
+                nc.scalar.copy(h[t][:, cols], h_bank[:])
+
+        out_rows = out.rearrange("(p t) n -> p t n", t=PACK)
+        gates = [keep.tile([P, S], F32, name=f"gate{t}") for t in range(PACK)]
+
+        def finish(t, c0, c1):
+            result = keep.tile([P, c1 - c0], F32, name=f"result{t}_{c0}")
+            nc.vector.tensor_tensor(result[:], h[t][:, c0:c1], gates[t][:, c0:c1], MULT)
+            nc.sync.dma_start(out_rows[:, t, c0:c1], result[:])
+
+        for t in range(PACK):
+            taken = []
+            for half in range(2):
+                entries = slice(half * HALF // GROUP, (half + 1) * HALF // GROUP)
+                at_n4 = keep.tile([P, HALF], F32, name=f"at_n4_{t}_{half}")
+                nc.vector.tensor_copy(at_n4[:], h[t][:].indirect(n4_sb[:, entries]))
+                taken.append(at_n4)
+            if 0 < t < PACK - 1:
+                finish(t - 1, 0, S)
+            for half in range(2):
+                cols = slice(half * HALF, (half + 1) * HALF)
+                entries = slice(half * HALF // GROUP, (half + 1) * HALF // GROUP)
+                diff = keep.tile([P, HALF], F32, name=f"diff{t}_{half}")
+                nc.vector.tensor_tensor(diff[:], h[t][:].indirect(n3_sb[:, entries]), taken[half][:], SUB)
+                nc.scalar.activation(out=gates[t][:, cols], in_=diff[:], func=SIGMOID)
+        finish(PACK - 2, 0, S)
+        finish(PACK - 1, 0, HALF)
+        finish(PACK - 1, HALF, S)

@@ -1,6 +1,7 @@
 from contextlib import ExitStack
 
 import concourse.mybir as mybir
+from concourse.masks import make_identity
 
 K, T, S, H, N = 512, 2048, 512, 512, 512
 FLOPS = 2 * S * (K * H + K * H + H * N)
@@ -21,6 +22,9 @@ P = 128
 PACK = 4
 GROUP = 16
 HALF = S // 2
+EARLY = 384
+SCALAR_SHARE = 48
+LATE = S - EARLY
 
 
 def tile_picked_twlcrossbcmp_none_p_kernel(
@@ -29,8 +33,7 @@ def tile_picked_twlcrossbcmp_none_p_kernel(
     nc = tc.nc
     with ExitStack() as ctx:
         keep = ctx.enter_context(tc.tile_pool(name="keep", bufs=1))
-        first_banks = ctx.enter_context(tc.psum_pool(name="first_banks", bufs=4))
-        second_banks = ctx.enter_context(tc.psum_pool(name="second_banks", bufs=4))
+        psum = ctx.enter_context(tc.psum_pool(name="psum", bufs=1))
 
         def list_tile(name):
             return keep.tile([P, S // GROUP], U16, name=name)
@@ -41,16 +44,10 @@ def tile_picked_twlcrossbcmp_none_p_kernel(
         table_words = keep.tile([P, T], U32, align_bytes=64)
         table_scales = keep.tile([P, T], U8, align_bytes=64)
         gain = keep.tile([P, PACK], F32)
-        pieces = [2, 2, 1]
-        raw = [
-            [keep.tile([P, PACK, H // pieces[i]], F32, name=f"raw{i}_{k}", align_bytes=64) for k in range(pieces[i])]
-            for i in range(3)
-        ]
+        raw = [keep.tile([P, PACK, H], F32, name=f"raw{i}", tag=f"raw{i}", align_bytes=64) for i in range(3)]
 
         def load_weights(i, w):
-            width = H // pieces[i]
-            for k in range(pieces[i]):
-                nc.sync.dma_start(raw[i][k][:], w.rearrange("(p j) c -> p j c", j=PACK)[:, :, k * width : (k + 1) * width])
+            nc.sync.dma_start(raw[i][:], w.rearrange("(p j) c -> p j c", j=PACK))
 
         warm = keep.tile([P, 8], F32)
 
@@ -60,11 +57,11 @@ def tile_picked_twlcrossbcmp_none_p_kernel(
 
         nc.sync.dma_start(table_words[:].bitcast(I32), x_words[0].rearrange("p n t -> p (n t)").bitcast(I32))
         nc.sync.dma_start(offs_sb[:], offs)
+        nc.sync.dma_start(two_sb[:], two)
         for q in range(4):
-            nc.scalar.dma_start(
+            nc.sync.dma_start(
                 table_scales[32 * q : 32 * q + 4, :].bitcast(I32), x_scales[0, 4 * q : 4 * q + 4, :].bitcast(I32)
             )
-        nc.sync.dma_start(two_sb[:], two)
         load_weights(0, w1)
         load_weights(1, w2)
         nc.sync.dma_start(gain[:], gn.rearrange("(p t) o -> p (t o)", t=PACK))
@@ -74,38 +71,39 @@ def tile_picked_twlcrossbcmp_none_p_kernel(
         nc.sync.dma_start(n4_sb[:], n4)
         nc.sync.dma_start(n3_sb[:], n3)
 
-        picked = []
-        for name, lst in (("x_offs", offs_sb), ("x_two", two_sb)):
-            words = keep.tile([P, S], U32, name=name + "_words", align_bytes=64)
-            scales = keep.tile([P, S], U8, name=name + "_scales", align_bytes=64)
-            nc.vector.tensor_copy(words[:], table_words[:].indirect(lst[:]))
-            picked.append((words, scales))
-        for (words, scales), lst in zip(picked, (offs_sb, two_sb)):
-            nc.vector.tensor_copy(scales[:], table_scales[:].indirect(lst[:]))
+        identity = keep.tile([P, P], F32)
+        make_identity(nc, identity[:])
 
-        dealt = [keep.tile([P, PACK, P, PACK], BF16, name=f"dealt{i}", align_bytes=64) for i in range(3)]
-        w_words = [keep.tile([P, PACK, P], U32, name=f"w_words{i}", align_bytes=64) for i in range(3)]
+        offs_words = keep.tile([P, S], U32, align_bytes=64)
+        offs_scales = keep.tile([P, S], U8, align_bytes=64)
+        two_words = keep.tile([P, S], U32, align_bytes=64)
+        nc.vector.tensor_copy(offs_words[:], table_words[:].indirect(offs_sb[:]))
+        nc.vector.tensor_copy(two_words[:], table_words[:].indirect(two_sb[:]))
+        nc.vector.tensor_copy(offs_scales[:], table_scales[:].indirect(offs_sb[:]))
+
+        dealt = {}
         w_scales = [keep.tile([P, PACK, P], U8, name=f"w_scales{i}", align_bytes=64) for i in range(3)]
 
-        def deal(i):
-            count = P // pieces[i]
-            for k in range(pieces[i]):
-                nc.scalar.copy(
-                    dealt[i][:, :, k * count : (k + 1) * count, :].rearrange("p t m j -> p m j t"),
-                    raw[i][k][:].rearrange("p j (m t) -> p m j t", t=PACK),
-                )
-
-        def quantize_weights(i, t0, t1):
-            nc.vector.quantize_mx(
-                out=w_words[i][:, t0:t1, :].rearrange("p t m -> p (t m)").bitcast(FP8X4),
-                scales=w_scales[i][:, t0:t1, :].rearrange("p t m -> p (t m)"),
-                in_=dealt[i][:, t0:t1, :, :].rearrange("p t m j -> p (t m j)"),
+        def deal(i, u, copy, m0=0, m1=P):
+            copy(
+                dealt[i, u][:].rearrange("p e m j -> p m j e")[:, m0:m1],
+                raw[i][:].rearrange("p j (m t) -> p m j t", t=PACK)[:, m0:m1, :, 2 * u : 2 * u + 2],
             )
 
-        def product(bank, i, t, words, scales):
+        def dealt_tile(i, u, tag):
+            dealt[i, u] = keep.tile([P, 2, P, PACK], BF16, name=f"dealt{i}_{u}", tag=tag, align_bytes=64)
+
+        def quantize_weights(i, t0, t1, words):
+            nc.vector.quantize_mx(
+                out=words.bitcast(FP8X4),
+                scales=w_scales[i][:, t0:t1, :].rearrange("p t m -> p (t m)"),
+                in_=dealt[i, t0 // 2][:, t0 % 2 : t0 % 2 + t1 - t0, :, :].rearrange("p e m j -> p (e m j)"),
+            )
+
+        def product(bank, w_words, i, t, words, scales):
             nc.tensor.matmul_mx(
                 out=bank,
-                lhsT=w_words[i][:, t, :].bitcast(FP8X4),
+                lhsT=w_words.bitcast(FP8X4),
                 lhsT_scale=w_scales[i][:, t, :],
                 rhs=words.bitcast(FP8X4),
                 rhs_scale=scales,
@@ -113,76 +111,146 @@ def tile_picked_twlcrossbcmp_none_p_kernel(
                 stop=True,
             )
 
-        deal(0)
-        quantize_weights(0, 0, PACK)
-        deal(1)
-        quantize_weights(1, 0, 1)
-        quantize_weights(1, 1, 2)
-        quantize_weights(1, 2, PACK)
+        def block(t):
+            return slice(t * P, (t + 1) * P)
+
+        w1_first = keep.tile([P, 2 * P], U32, align_bytes=64)
+        w2_words = keep.tile([P, H], U32, tag="w2_then_w3", align_bytes=64)
+        dealt_tile(0, 0, "two_scales")
+        dealt_tile(0, 1, "dealt0_1")
+        dealt_tile(1, 0, "dealt1_0")
+        deal(0, 0, nc.scalar.copy)
+        deal(0, 1, nc.scalar.copy)
+        quantize_weights(0, 0, 2, w1_first[:])
+        two_scales = keep.tile([P, S], U8, tag="two_scales", align_bytes=64)
+        nc.vector.tensor_copy(two_scales[:], table_scales[:].indirect(two_sb[:]))
+        deal(1, 0, nc.scalar.copy, 0, SCALAR_SHARE)
+        deal(1, 0, nc.vector.tensor_copy, SCALAR_SHARE, P)
+        quantize_weights(1, 0, 1, w2_words[:, 0:P])
+        quantize_weights(1, 1, 2, w2_words[:, P : 2 * P])
+        dealt_tile(1, 1, "dealt1_0")
+        deal(1, 1, nc.scalar.copy, 0, SCALAR_SHARE)
+        deal(1, 1, nc.vector.tensor_copy, SCALAR_SHARE, P)
+        w1_second = keep.tile([P, 2 * P], U32, tag="raw1", align_bytes=64)
+        quantize_weights(0, 2, PACK, w1_second[:])
+        quantize_weights(1, 2, PACK, w2_words[:, 2 * P : H])
 
         y = [keep.tile([P, S], F32, name=f"y{t}") for t in range(PACK)]
         d = [keep.tile([P, S], F32, name=f"d{t}") for t in range(PACK)]
+        minus_d = [keep.tile([P, EARLY], F32, name=f"minus_d{t}", tag=f"minus_d{t}") for t in range(PACK)]
+
         for t in range(PACK):
-            y_bank = first_banks.tile([P, S], F32, name="first_bank")
-            product(y_bank[:], 0, t, picked[0][0][:], picked[0][1][:])
+            y_bank = psum.tile([P, S], F32, name="y_bank", tag="bank0")
+            product(y_bank[:], (w1_first, w1_second)[t // 2][:, block(t % 2)], 0, t, offs_words[:], offs_scales[:])
             nc.scalar.activation(out=y[t][:], in_=y_bank[:], func=COPY, scale=gain[:, t : t + 1])
-            d_bank = first_banks.tile([P, S], F32, name="first_bank")
-            product(d_bank[:], 1, t, picked[1][0][:], picked[1][1][:])
+            d_bank = psum.tile([P, S], F32, name="d_bank", tag=f"bank{t + 1}")
+            product(d_bank[:], w2_words[:, block(t)], 1, t, two_words[:], two_scales[:])
+            nc.scalar.activation(out=minus_d[t][:], in_=d_bank[:, 0:EARLY], func=COPY, scale=-0.75)
             nc.scalar.activation(out=d[t][:], in_=d_bank[:], func=COPY, scale=0.75)
 
-        deal(2)
+        dealt_tile(2, 0, "w2_then_w3")
+        deal(2, 0, nc.scalar.copy)
 
         h = [keep.tile([P, S], F32, name=f"h{t}") for t in range(PACK)]
-        for half in range(2):
-            cols = slice(half * HALF, (half + 1) * HALF)
-            entries = slice(half * HALF // GROUP, (half + 1) * HALF // GROUP)
-            left = keep.tile([P, PACK, HALF], F32, name=f"left{half}")
-            right = keep.tile([P, PACK, HALF], F32, name=f"right{half}")
-            for t in range(PACK):
-                nc.vector.tensor_tensor(left[:, t, :], d[t][:].indirect(n2_sb[:, entries]), y[t][:, cols], MULT)
-                nc.vector.tensor_tensor(right[:, t, :], y[t][:].indirect(n1_sb[:, entries]), d[t][:, cols], MULT)
-            z = keep.tile([P, HALF, PACK], BF16, name=f"z{half}", align_bytes=64)
-            nc.vector.tensor_tensor(
-                z[:].rearrange("p (c i) t -> p c t i", i=4),
-                left[:].rearrange("p t (c i) -> p c t i", i=4),
-                right[:].rearrange("p t (c i) -> p c t i", i=4),
-                SUB,
+        z_words = keep.tile([P, S], U32, align_bytes=64)
+        z_scales = keep.tile([P, S], U8, align_bytes=64)
+        halves = [slice(0, HALF), slice(HALF, S)]
+        entries = [slice(0, HALF // GROUP), slice(HALF // GROUP, S // GROUP)]
+
+        early, late = slice(0, EARLY), slice(EARLY, S)
+        early_entries, late_entries = slice(0, EARLY // GROUP), slice(EARLY // GROUP, S // GROUP)
+        blocks = EARLY // P
+        spans = [(0, 2), (2, blocks)]
+        z_rows = keep.tile([P, blocks * PACK * P], BF16, tag="z_rows", align_bytes=64)
+        rows_view = z_rows[:].rearrange("j (b u p e) -> j b u p e", u=2, p=P, e=2)
+        for u in range(2):
+            turned = [
+                psum.tile([P, b1 - b0, 2, P], F32, name=f"turned{u}_{b0}", tag=tag)
+                for (b0, b1), tag in zip(spans, (("bank0", "bank3"), ("bank1", "bank2"))[u])
+            ]
+            for e in range(2):
+                t = 2 * u + e
+                left = keep.tile([P, EARLY], F32, name=f"left{t}")
+                right = keep.tile([P, EARLY], F32, name=f"right{t}")
+                nc.vector.tensor_tensor(right[:], y[t][:].indirect(n1_sb[:, early_entries]), minus_d[t][:], MULT)
+                nc.vector.tensor_tensor(left[:], d[t][:].indirect(n2_sb[:, early_entries]), y[t][:, early], MULT)
+                for bank, (b0, b1) in zip(turned, spans):
+                    for b in range(b0, b1):
+                        sums = bank[:, b - b0, e, :]
+                        nc.tensor.matmul(sums, right[:, block(b)], identity[:], start=True, stop=False, is_transpose=True)
+                        nc.tensor.matmul(sums, left[:, block(b)], identity[:], start=False, stop=True, is_transpose=True)
+            for bank, (b0, b1) in zip(turned, spans):
+                nc.scalar.copy(rows_view[:, b0:b1, u, :, :], bank[:].rearrange("j b e p -> j b p e"))
+        z_early = [
+            keep.tile([P, (b1 - b0) * PACK * P], BF16, name=f"z_early{b0}", tag=f"z_early{b0}", align_bytes=64)
+            for b0, b1 in spans
+        ]
+        pairs = z_rows[:].bitcast(F32)
+        for z_part, (b0, b1), tag in zip(z_early, spans, ("bank4", "bank5")):
+            back = psum.tile([P, b1 - b0, 2, P], F32, name="back", tag=tag)
+            for b in range(b0, b1):
+                for u in range(2):
+                    nc.tensor.transpose(back[:, b - b0, u, :], pairs[:, block(2 * b + u)], identity[:])
+            nc.scalar.copy(
+                z_part[:].bitcast(F32).rearrange("p (b j u) -> p b j u", j=P, u=2),
+                back[:].rearrange("p b u j -> p b j u"),
             )
-            if half == 0:
-                quantize_weights(2, 0, PACK)
-            z_words = keep.tile([P, HALF], U32, name=f"z_words{half}", align_bytes=64)
-            z_scales = keep.tile([P, HALF], U8, name=f"z_scales{half}", align_bytes=64)
-            nc.vector.quantize_mx(
-                out=z_words[:].bitcast(FP8X4), scales=z_scales[:], in_=z[:].rearrange("p n t -> p (n t)")
-            )
-            for t in range(PACK):
-                h_bank = second_banks.tile([P, HALF], F32, name="second_bank")
-                product(h_bank[:], 2, t, z_words[:], z_scales[:])
-                nc.scalar.copy(h[t][:, cols], h_bank[:])
+        dealt_tile(2, 1, "z_rows")
+        deal(2, 1, nc.scalar.copy)
+
+        products = keep.tile([P, 2, PACK, LATE], F32, tag=f"minus_d{PACK - 1}")
+        for t in range(PACK):
+            nc.vector.tensor_tensor(products[:, 0, t, :], d[t][:].indirect(n2_sb[:, late_entries]), y[t][:, late], MULT)
+            nc.vector.tensor_tensor(products[:, 1, t, :], y[t][:].indirect(n1_sb[:, late_entries]), d[t][:, late], MULT)
+        w3_first = keep.tile([P, P], U32, align_bytes=64)
+        quantize_weights(2, 0, 1, w3_first[:])
+
+        def quantize_early(n):
+            cols = slice(spans[n][0] * P, spans[n][1] * P)
+            nc.vector.quantize_mx(out=z_words[:, cols].bitcast(FP8X4), scales=z_scales[:, cols], in_=z_early[n][:])
+
+        quantize_early(0)
+        z_late = keep.tile([P, LATE, PACK], BF16, tag="z_early0", align_bytes=64)
+        both = products[:].rearrange("p s t (c i) -> p s c t i", i=4)
+        nc.vector.tensor_tensor(z_late[:].rearrange("p (c i) t -> p c t i", i=4), both[:, 0], both[:, 1], SUB)
+        quantize_early(1)
+        nc.vector.quantize_mx(
+            out=z_words[:, late].bitcast(FP8X4),
+            scales=z_scales[:, late],
+            in_=z_late[:].rearrange("p n t -> p (n t)"),
+        )
+        for cols, tag in ((slice(0, 2 * P), "bank6"), (slice(2 * P, EARLY), "bank7"), (late, "bank3")):
+            h_bank = psum.tile([P, cols.stop - cols.start], F32, name="h_first", tag=tag)
+            product(h_bank[:], w3_first[:], 2, 0, z_words[:, cols], z_scales[:, cols])
+            nc.scalar.copy(h[0][:, cols], h_bank[:])
+        w3_rest = keep.tile([P, H - P], U32, tag="z_early0", align_bytes=64)
+        quantize_weights(2, 1, 2, w3_rest[:, 0:P])
+        quantize_weights(2, 2, PACK, w3_rest[:, P : H - P])
+        for t, tag in zip(range(1, PACK), ("bank0", "bank1", "bank2")):
+            h_bank = psum.tile([P, S], F32, name="h_rest", tag=tag)
+            product(h_bank[:], w3_rest[:, block(t - 1)], 2, t, z_words[:], z_scales[:])
+            nc.scalar.copy(h[t][:, 0:S], h_bank[:])
 
         out_rows = out.rearrange("(p t) n -> p t n", t=PACK)
         gates = [keep.tile([P, S], F32, name=f"gate{t}") for t in range(PACK)]
 
-        def finish(t, c0, c1):
-            result = keep.tile([P, c1 - c0], F32, name=f"result{t}_{c0}")
-            nc.vector.tensor_tensor(result[:], h[t][:, c0:c1], gates[t][:, c0:c1], MULT)
-            nc.sync.dma_start(out_rows[:, t, c0:c1], result[:])
+        def finish(t, cols):
+            result = keep.tile([P, cols.stop - cols.start], F32, name=f"result{t}_{cols.start}")
+            nc.vector.tensor_tensor(result[:], h[t][:, cols], gates[t][:, cols], MULT)
+            nc.sync.dma_start(out_rows[:, t, cols], result[:])
 
+        whole = slice(0, S)
         for t in range(PACK):
-            taken = []
-            for half in range(2):
-                entries = slice(half * HALF // GROUP, (half + 1) * HALF // GROUP)
-                at_n4 = keep.tile([P, HALF], F32, name=f"at_n4_{t}_{half}")
-                nc.vector.tensor_copy(at_n4[:], h[t][:].indirect(n4_sb[:, entries]))
-                taken.append(at_n4)
+            at_n4 = keep.tile([P, S], F32, name=f"at_n4_{t}")
+            for cols, listed in zip(halves, entries):
+                nc.vector.tensor_copy(at_n4[:, cols], h[t][:].indirect(n4_sb[:, listed]))
             if 0 < t < PACK - 1:
-                finish(t - 1, 0, S)
-            for half in range(2):
-                cols = slice(half * HALF, (half + 1) * HALF)
-                entries = slice(half * HALF // GROUP, (half + 1) * HALF // GROUP)
-                diff = keep.tile([P, HALF], F32, name=f"diff{t}_{half}")
-                nc.vector.tensor_tensor(diff[:], h[t][:].indirect(n3_sb[:, entries]), taken[half][:], SUB)
-                nc.scalar.activation(out=gates[t][:, cols], in_=diff[:], func=SIGMOID)
-        finish(PACK - 2, 0, S)
-        finish(PACK - 1, 0, HALF)
-        finish(PACK - 1, HALF, S)
+                finish(t - 1, whole)
+            diff = keep.tile([P, S], F32, name=f"diff{t}")
+            for cols, listed in zip(halves, entries):
+                nc.vector.tensor_tensor(diff[:, cols], h[t][:].indirect(n3_sb[:, listed]), at_n4[:, cols], SUB)
+            for cols in halves if t == PACK - 1 else [whole]:
+                nc.scalar.activation(out=gates[t][:, cols], in_=diff[:, cols], func=SIGMOID)
+        finish(PACK - 2, whole)
+        finish(PACK - 1, halves[0])
+        finish(PACK - 1, halves[1])

@@ -234,23 +234,22 @@ def tile_picked_twlcrossbcmp_none_p_kernel(
         out_rows = out.rearrange("(p t) n -> p t n", t=PACK)
         gates = [keep.tile([P, S], F32, name=f"gate{t}") for t in range(PACK)]
 
-        def finish(t, cols):
-            result = keep.tile([P, cols.stop - cols.start], F32, name=f"result{t}_{cols.start}")
-            nc.vector.tensor_tensor(result[:], h[t][:, cols], gates[t][:, cols], MULT)
+        def finish(t, cols, engine, tag):
+            result = keep.tile([P, cols.stop - cols.start], F32, name=f"result{t}_{cols.start}", tag=tag)
+            engine.tensor_tensor(result[:], h[t][:, cols], gates[t][:, cols], MULT)
             nc.sync.dma_start(out_rows[:, t, cols], result[:])
 
         whole = slice(0, S)
         for t in range(PACK):
-            at_n4 = keep.tile([P, S], F32, name=f"at_n4_{t}")
-            for cols, listed in zip(halves, entries):
-                nc.vector.tensor_copy(at_n4[:, cols], h[t][:].indirect(n4_sb[:, listed]))
+            at_n4 = [keep.tile([P, HALF], F32, name=f"at_n4_{t}_{n}", tag=f"at_n4_{n}") for n in range(2)]
+            for n in range(2):
+                nc.vector.tensor_copy(at_n4[n][:], h[t][:].indirect(n4_sb[:, entries[n]]))
+            for n in range(2):
+                diff = keep.tile([P, HALF], F32, name=f"diff{t}_{n}", tag=f"diff{t}_{n}")
+                nc.vector.tensor_tensor(diff[:], h[t][:].indirect(n3_sb[:, entries[n]]), at_n4[n][:], SUB)
+                nc.scalar.activation(out=gates[t][:, halves[n]], in_=diff[:], func=SIGMOID)
             if 0 < t < PACK - 1:
-                finish(t - 1, whole)
-            diff = keep.tile([P, S], F32, name=f"diff{t}")
-            for cols, listed in zip(halves, entries):
-                nc.vector.tensor_tensor(diff[:, cols], h[t][:].indirect(n3_sb[:, listed]), at_n4[:, cols], SUB)
-            for cols in halves if t == PACK - 1 else [whole]:
-                nc.scalar.activation(out=gates[t][:, cols], in_=diff[:, cols], func=SIGMOID)
-        finish(PACK - 2, whole)
-        finish(PACK - 1, halves[0])
-        finish(PACK - 1, halves[1])
+                finish(t - 1, whole, nc.gpsimd, f"diff{t}_0")
+        finish(PACK - 2, whole, nc.vector, "result2")
+        finish(PACK - 1, halves[0], nc.vector, "result3_first")
+        finish(PACK - 1, halves[1], nc.vector, "result3_second")

@@ -248,8 +248,13 @@ def tile_picked_twlcrossbcmp_none_p_kernel(
                 diff = keep.tile([P, HALF], F32, name=f"diff{t}_{n}", tag=f"diff{t}_{n}")
                 nc.vector.tensor_tensor(diff[:], h[t][:].indirect(n3_sb[:, entries[n]]), at_n4[n][:], SUB)
                 nc.scalar.activation(out=gates[t][:, halves[n]], in_=diff[:], func=SIGMOID)
-            if 0 < t < PACK - 1:
-                finish(t - 1, whole, nc.gpsimd, f"diff{t}_0")
+            if t == 0:
+                finish(0, halves[0], nc.gpsimd, "result0_first")
+            if t == 1:
+                finish(0, halves[1], nc.gpsimd, "diff1_0")
+                finish(1, slice(0, P), nc.gpsimd, "result1_first")
+            if t == 2:
+                finish(1, slice(P, S), nc.gpsimd, "diff2_0")
         finish(PACK - 2, whole, nc.vector, "result2")
         finish(PACK - 1, halves[0], nc.vector, "result3_first")
         finish(PACK - 1, halves[1], nc.vector, "result3_second")

from contextlib import ExitStack

import concourse.mybir as mybir
from concourse.masks import make_identity

K, T, S, H, N = 512, 2048, 512, 512, 512
FLOPS = 2 * S * (K * H + K * H + H * N)

F32 = mybir.dt.float32
BF16 = mybir.dt.bfloat16
I32 = mybir.dt.int32
U32 = mybir.dt.uint32
U16 = mybir.dt.uint16
U8 = mybir.dt.uint8
FP8X4 = mybir.dt.float8_e4m3fn_x4
MULT = mybir.AluOpType.mult
SUB = mybir.AluOpType.subtract
COPY = mybir.ActivationFunctionType.Copy
SIGMOID = mybir.ActivationFunctionType.Sigmoid

P = 128
PACK = 4
GROUP = 16
HALF = S // 2
EARLY = 384
SCALAR_SHARE = 48
LATE = S - EARLY


def tile_picked_twlcrossbcmp_none_p_kernel(
    tc, x_words, x_scales, w1, w2, gn, w3, offs, two, n1, n2, n3, n4, out
):
    nc = tc.nc
    with ExitStack() as ctx:
        keep = ctx.enter_context(tc.tile_pool(name="keep", bufs=1))
        psum = ctx.enter_context(tc.psum_pool(name="psum", bufs=1))

        def list_tile(name):
            return keep.tile([P, S // GROUP], U16, name=name)

        offs_sb, two_sb = list_tile("offs_sb"), list_tile("two_sb")
        n1_sb, n2_sb, n3_sb, n4_sb = list_tile("n1_sb"), list_tile("n2_sb"), list_tile("n3_sb"), list_tile("n4_sb")

        table_words = keep.tile([P, T], U32, align_bytes=64)
        table_scales = keep.tile([P, T], U8, align_bytes=64)
        gain = keep.tile([P, PACK], F32)
        raw = [keep.tile([P, PACK, H], F32, name=f"raw{i}", tag=f"raw{i}", align_bytes=64) for i in range(3)]

        def load_weights(i, w):
            nc.sync.dma_start(raw[i][:], w.rearrange("(p j) c -> p j c", j=PACK))

        warm = keep.tile([P, 8], F32)

        nc.vector.memset(table_scales[:].bitcast(I32), 0)
        nc.vector.memset(warm[:, 0:1], 0.0)
        nc.scalar.activation(out=warm[:, 4:5], in_=warm[:, 0:1], func=SIGMOID)

        nc.sync.dma_start(table_words[:].bitcast(I32), x_words[0].rearrange("p n t -> p (n t)").bitcast(I32))
        nc.sync.dma_start(offs_sb[:], offs)
        nc.sync.dma_start(two_sb[:], two)
        for q in range(4):
            nc.sync.dma_start(
                table_scales[32 * q : 32 * q + 4, :].bitcast(I32), x_scales[0, 4 * q : 4 * q + 4, :].bitcast(I32)
            )
        load_weights(0, w1)
        load_weights(1, w2)
        nc.sync.dma_start(gain[:], gn.rearrange("(p t) o -> p (t o)", t=PACK))
        nc.sync.dma_start(n2_sb[:], n2)
        nc.sync.dma_start(n1_sb[:], n1)
        load_weights(2, w3)
        nc.sync.dma_start(n4_sb[:], n4)
        nc.sync.dma_start(n3_sb[:], n3)

        identity = keep.tile([P, P], F32)
        make_identity(nc, identity[:])

        offs_words = keep.tile([P, S], U32, align_bytes=64)
        offs_scales = keep.tile([P, S], U8, align_bytes=64)
        two_words = keep.tile([P, S], U32, align_bytes=64)
        nc.vector.tensor_copy(offs_words[:], table_words[:].indirect(offs_sb[:]))
        nc.vector.tensor_copy(two_words[:], table_words[:].indirect(two_sb[:]))
        nc.vector.tensor_copy(offs_scales[:], table_scales[:].indirect(offs_sb[:]))

        dealt = {}
        w_scales = [keep.tile([P, PACK, P], U8, name=f"w_scales{i}", align_bytes=64) for i in range(3)]

        def deal(i, u, copy, m0=0, m1=P):
            copy(
                dealt[i, u][:].rearrange("p e m j -> p m j e")[:, m0:m1],
                raw[i][:].rearrange("p j (m t) -> p m j t", t=PACK)[:, m0:m1, :, 2 * u : 2 * u + 2],
            )

        def dealt_tile(i, u, tag):
            dealt[i, u] = keep.tile([P, 2, P, PACK], BF16, name=f"dealt{i}_{u}", tag=tag, align_bytes=64)

        def quantize_weights(i, t0, t1, words):
            nc.vector.quantize_mx(
                out=words.bitcast(FP8X4),
                scales=w_scales[i][:, t0:t1, :].rearrange("p t m -> p (t m)"),
                in_=dealt[i, t0 // 2][:, t0 % 2 : t0 % 2 + t1 - t0, :, :].rearrange("p e m j -> p (e m j)"),
            )

        def product(bank, w_words, i, t, words, scales):
            nc.tensor.matmul_mx(
                out=bank,
                lhsT=w_words.bitcast(FP8X4),
                lhsT_scale=w_scales[i][:, t, :],
                rhs=words.bitcast(FP8X4),
                rhs_scale=scales,
                start=True,
                stop=True,
            )

        def block(t):
            return slice(t * P, (t + 1) * P)

        w1_first = keep.tile([P, 2 * P], U32, align_bytes=64)
        w2_words = keep.tile([P, H], U32, tag="w2_then_w3", align_bytes=64)
        dealt_tile(0, 0, "two_scales")
        dealt_tile(0, 1, "dealt0_1")
        dealt_tile(1, 0, "dealt1_0")
        deal(0, 0, nc.scalar.copy)
        deal(0, 1, nc.scalar.copy)
        quantize_weights(0, 0, 2, w1_first[:])
        two_scales = keep.tile([P, S], U8, tag="two_scales", align_bytes=64)
        nc.vector.tensor_copy(two_scales[:], table_scales[:].indirect(two_sb[:]))
        deal(1, 0, nc.scalar.copy, 0, SCALAR_SHARE)
        deal(1, 0, nc.vector.tensor_copy, SCALAR_SHARE, P)
        quantize_weights(1, 0, 1, w2_words[:, 0:P])
        quantize_weights(1, 1, 2, w2_words[:, P : 2 * P])
        dealt_tile(1, 1, "dealt1_0")
        deal(1, 1, nc.scalar.copy, 0, SCALAR_SHARE)
        deal(1, 1, nc.vector.tensor_copy, SCALAR_SHARE, P)
        w1_second = keep.tile([P, 2 * P], U32, tag="raw1", align_bytes=64)
        quantize_weights(0, 2, PACK, w1_second[:])
        quantize_weights(1, 2, PACK, w2_words[:, 2 * P : H])

        y = [keep.tile([P, S], F32, name=f"y{t}") for t in range(PACK)]
        d = [keep.tile([P, S], F32, name=f"d{t}") for t in range(PACK)]
        minus_d = [keep.tile([P, EARLY], F32, name=f"minus_d{t}", tag=f"minus_d{t}") for t in range(PACK)]

        for t in range(PACK):
            y_bank = psum.tile([P, S], F32, name="y_bank", tag="bank0")
            product(y_bank[:], (w1_first, w1_second)[t // 2][:, block(t % 2)], 0, t, offs_words[:], offs_scales[:])
            nc.scalar.activation(out=y[t][:], in_=y_bank[:], func=COPY, scale=gain[:, t : t + 1])
            d_bank = psum.tile([P, S], F32, name="d_bank", tag=f"bank{t + 1}")
            product(d_bank[:], w2_words[:, block(t)], 1, t, two_words[:], two_scales[:])
            nc.scalar.activation(out=minus_d[t][:], in_=d_bank[:, 0:EARLY], func=COPY, scale=-0.75)
            nc.scalar.activation(out=d[t][:], in_=d_bank[:], func=COPY, scale=0.75)

        dealt_tile(2, 0, "w2_then_w3")
        deal(2, 0, nc.scalar.copy)

        h = [keep.tile([P, S], F32, name=f"h{t}") for t in range(PACK)]
        z_words = keep.tile([P, S], U32, align_bytes=64)
        z_scales = keep.tile([P, S], U8, align_bytes=64)
        halves = [slice(0, HALF), slice(HALF, S)]
        entries = [slice(0, HALF // GROUP), slice(HALF // GROUP, S // GROUP)]

        early, late = slice(0, EARLY), slice(EARLY, S)
        early_entries, late_entries = slice(0, EARLY // GROUP), slice(EARLY // GROUP, S // GROUP)
        blocks = EARLY // P
        spans = [(0, 2), (2, blocks)]
        z_rows = keep.tile([P, blocks * PACK * P], BF16, tag="z_rows", align_bytes=64)
        rows_view = z_rows[:].rearrange("j (b u p e) -> j b u p e", u=2, p=P, e=2)
        for u in range(2):
            turned = [
                psum.tile([P, b1 - b0, 2, P], F32, name=f"turned{u}_{b0}", tag=tag)
                for (b0, b1), tag in zip(spans, (("bank0", "bank3"), ("bank1", "bank2"))[u])
            ]
            for e in range(2):
                t = 2 * u + e
                left = keep.tile([P, EARLY], F32, name=f"left{t}")
                right = keep.tile([P, EARLY], F32, name=f"right{t}")
                nc.vector.tensor_tensor(right[:], y[t][:].indirect(n1_sb[:, early_entries]), minus_d[t][:], MULT)
                nc.vector.tensor_tensor(left[:], d[t][:].indirect(n2_sb[:, early_entries]), y[t][:, early], MULT)
                for bank, (b0, b1) in zip(turned, spans):
                    for b in range(b0, b1):
                        sums = bank[:, b - b0, e, :]
                        nc.tensor.matmul(sums, right[:, block(b)], identity[:], start=True, stop=False, is_transpose=True)
                        nc.tensor.matmul(sums, left[:, block(b)], identity[:], start=False, stop=True, is_transpose=True)
            for bank, (b0, b1) in zip(turned, spans):
                nc.scalar.copy(rows_view[:, b0:b1, u, :, :], bank[:].rearrange("j b e p -> j b p e"))
        z_early = [
            keep.tile([P, (b1 - b0) * PACK * P], BF16, name=f"z_early{b0}", tag=f"z_early{b0}", align_bytes=64)
            for b0, b1 in spans
        ]
        pairs = z_rows[:].bitcast(F32)
        for z_part, (b0, b1), tag in zip(z_early, spans, ("bank4", "bank5")):
            back = psum.tile([P, b1 - b0, 2, P], F32, name="back", tag=tag)
            for b in range(b0, b1):
                for u in range(2):
                    nc.tensor.transpose(back[:, b - b0, u, :], pairs[:, block(2 * b + u)], identity[:])
            nc.scalar.copy(
                z_part[:].bitcast(F32).rearrange("p (b j u) -> p b j u", j=P, u=2),
                back[:].rearrange("p b u j -> p b j u"),
            )
        dealt_tile(2, 1, "z_rows")
        deal(2, 1, nc.scalar.copy)

        products = keep.tile([P, 2, PACK, LATE], F32, tag=f"minus_d{PACK - 1}")
        for t in range(PACK):
            nc.vector.tensor_tensor(products[:, 0, t, :], d[t][:].indirect(n2_sb[:, late_entries]), y[t][:, late], MULT)
            nc.vector.tensor_tensor(products[:, 1, t, :], y[t][:].indirect(n1_sb[:, late_entries]), d[t][:, late], MULT)
        w3_first = keep.tile([P, P], U32, align_bytes=64)
        quantize_weights(2, 0, 1, w3_first[:])

        def quantize_early(n):
            cols = slice(spans[n][0] * P, spans[n][1] * P)
            nc.vector.quantize_mx(out=z_words[:, cols].bitcast(FP8X4), scales=z_scales[:, cols], in_=z_early[n][:])

        quantize_early(0)
        z_late = keep.tile([P, LATE, PACK], BF16, tag="z_early0", align_bytes=64)
        both = products[:].rearrange("p s t (c i) -> p s c t i", i=4)
        nc.vector.tensor_tensor(z_late[:].rearrange("p (c i) t -> p c t i", i=4), both[:, 0], both[:, 1], SUB)
        quantize_early(1)
        nc.vector.quantize_mx(
            out=z_words[:, late].bitcast(FP8X4),
            scales=z_scales[:, late],
            in_=z_late[:].rearrange("p n t -> p (n t)"),
        )
        for cols, tag in ((slice(0, 2 * P), "bank6"), (slice(2 * P, EARLY), "bank7"), (late, "bank3")):
            h_bank = psum.tile([P, cols.stop - cols.start], F32, name="h_first", tag=tag)
            product(h_bank[:], w3_first[:], 2, 0, z_words[:, cols], z_scales[:, cols])
            nc.scalar.copy(h[0][:, cols], h_bank[:])
        w3_rest = keep.tile([P, H - P], U32, tag="z_early0", align_bytes=64)
        quantize_weights(2, 1, 2, w3_rest[:, 0:P])
        quantize_weights(2, 2, PACK, w3_rest[:, P : H - P])
        for t, tag in zip(range(1, PACK), ("bank0", "bank1", "bank2")):
            h_bank = psum.tile([P, S], F32, name="h_rest", tag=tag)
            product(h_bank[:], w3_rest[:, block(t - 1)], 2, t, z_words[:], z_scales[:])
            nc.scalar.copy(h[t][:, 0:S], h_bank[:])

        out_rows = out.rearrange("(p t) n -> p t n", t=PACK)
        gates = [keep.tile([P, S], F32, name=f"gate{t}") for t in range(PACK)]

        def finish(t, cols, engine, tag):
            result = keep.tile([P, cols.stop - cols.start], F32, name=f"result{t}_{cols.start}", tag=tag)
            engine.tensor_tensor(result[:], h[t][:, cols], gates[t][:, cols], MULT)
            nc.sync.dma_start(out_rows[:, t, cols], result[:])

        whole = slice(0, S)
        for t in range(PACK):
            at_n4 = [keep.tile([P, HALF], F32, name=f"at_n4_{t}_{n}", tag=f"at_n4_{n}") for n in range(2)]
            for n in range(2):
                nc.vector.tensor_copy(at_n4[n][:], h[t][:].indirect(n4_sb[:, entries[n]]))
            for n in range(2):
                diff = keep.tile([P, HALF], F32, name=f"diff{t}_{n}", tag=f"diff{t}_{n}")
                nc.vector.tensor_tensor(diff[:], h[t][:].indirect(n3_sb[:, entries[n]]), at_n4[n][:], SUB)
                nc.scalar.activation(out=gates[t][:, halves[n]], in_=diff[:], func=SIGMOID)
            if t == 0:
                finish(0, halves[0], nc.gpsimd, "result0_first")
            if t == 1:
                finish(0, halves[1], nc.gpsimd, "diff1_0")
                finish(1, slice(0, P), nc.gpsimd, "result1_first")
            if t == 2:
                finish(1, slice(P, S), nc.gpsimd, "diff2_0")
        finish(PACK - 2, whole, nc.vector, "result2")
        finish(PACK - 1, halves[0], nc.vector, "result3_first")
        finish(PACK - 1, halves[1], nc.vector, "result3_second")
